import numpy as np
import ml_dtypes


def mxq(x, axis, fmt="e4m3"):
    dtype, down = {"e4m3": (ml_dtypes.float8_e4m3fn, 7), "e5m2": (ml_dtypes.float8_e5m2, 14)}[fmt]
    v = np.moveaxis(np.asarray(x, np.float32).astype(ml_dtypes.bfloat16).astype(np.float64), axis, -1)
    blocks = v.reshape(v.shape[:-1] + (-1, 32))
    amax = np.abs(blocks).max(-1, keepdims=True)
    byte = np.maximum(np.where(amax > 0, np.frexp(amax)[1] - 1 + 127, 0) - down, 1)
    scale = np.exp2(byte - 127.0)
    codes = (blocks / scale).astype(np.float32).astype(dtype).astype(np.float64)
    return np.moveaxis((codes * scale).reshape(v.shape), -1, axis)


WIDE = False


def mx_kscale(k):
    if not WIDE:
        return np.ones(k)
    levels = np.array([30, -30])
    if k % 512:
        return np.exp2(np.random.permutation(np.resize(levels, k // 32))).repeat(32)
    a = np.empty((k // 512, 16))
    for p in range(k // 512):
        a[p, :8] = np.random.permutation(np.resize(levels, 8))
        for g in range(8):
            far = levels[np.abs(levels - a[p, g]) >= 10]
            a[p, g + 8] = far[np.random.randint(len(far))]
    return np.exp2(a.ravel()).repeat(32)


def f64(x):
    return np.asarray(x).astype(np.float64)


def striped(idx):
    return np.tile(idx.reshape(-1, 16).T, (8, 1)).astype(np.uint16)


def unstriped(offs):
    return offs[:16].T.reshape(-1).astype(np.int64)


E2M1 = np.array([0.0, 0.5, 1.0, 1.5, 2.0, 3.0, 4.0, 6.0, -0.0, -0.5, -1.0, -1.5, -2.0, -3.0, -4.0, -6.0])


def pack_weight(w, fmt):
    k, n = w.shape
    w = f64(np.asarray(w, np.float32).astype(ml_dtypes.bfloat16)).reshape(k // 32, 32, n)
    amax = np.abs(w).max(1)
    if fmt == "e4m3":
        byte = np.frexp(amax)[1] - 1 + 127 - 7
    else:
        mant, ex = np.frexp(amax / 6.0)
        byte = np.where(mant > 0.5, ex, ex - 1) + 127
    byte = np.clip(np.where(amax > 0, byte, 1), 1, 254)
    scaled = (w * np.exp2(127.0 - byte)[:, None, :]).reshape(k, n).astype(np.float32)
    by_word = np.ascontiguousarray(scaled.reshape(k // 512, 128, 4, n).transpose(0, 1, 3, 2))
    if fmt == "e4m3":
        words = by_word.astype(ml_dtypes.float8_e4m3fn).view(np.uint8)
    else:
        c = by_word.astype(ml_dtypes.float4_e2m1fn).view(np.uint8) & 0xF
        words = (c[..., 0::2] | (c[..., 1::2] << 4)).reshape(k // 512, 128, 2 * n)
    return np.ascontiguousarray(words), np.ascontiguousarray(byte.astype(np.uint8).reshape(k // 512, 16, n))


def unpack_weight(words, scales, fmt):
    g, _, n = scales.shape
    words = np.ascontiguousarray(words).reshape(g, 128, n, -1)
    if fmt == "e4m3":
        vals = words.view(ml_dtypes.float8_e4m3fn).astype(np.float64)
    else:
        nib = np.empty((g, 128, n, 4), np.uint8)
        nib[..., 0::2] = words & 0xF
        nib[..., 1::2] = words >> 4
        vals = E2M1[nib]
    vals = vals * np.repeat(np.exp2(scales.astype(np.float64) - 127.0), 8, axis=1)[..., None]
    return vals.transpose(0, 1, 3, 2).reshape(g * 512, n)


K, T, E, C, N = 128, 2048, 8, 512, 512


def by_expert(wq, xq):
    return np.concatenate([wq[e].T @ xq[:, e * C:(e + 1) * C] for e in range(E)], axis=1)


def setup_inputs():
    n = np.random.standard_normal
    s = mx_kscale(N)[:, None]
    first = np.random.permutation(np.repeat(np.arange(E), T // E))
    second = (first + 1 + np.random.permutation(np.repeat(np.arange(E - 1), -(-T // (E - 1)))[:T])) % E
    while np.bincount(second, minlength=E).max() != T // E:
        load = np.bincount(second, minlength=E); hi, lo = int(load.argmax()), int(load.argmin())
        t = np.flatnonzero((second == hi) & (first != lo))[0]; second[t] = lo
    slot_token = np.empty(E * C, np.int64); pos = np.empty((2, T), np.int64); fill = np.zeros(E, np.int64)
    place = np.stack([np.random.permutation(C) for _ in range(E)])
    for r, deal in enumerate((first, second)):
        for t in np.random.permutation(T):
            e = deal[t]; j = e * C + place[e, fill[e]]; fill[e] += 1; slot_token[j] = t; pos[r, t] = j
    g = np.random.uniform(0.2, 0.8, T)
    w_slot = np.empty(E * C); w_slot[pos[0]] = g; w_slot[pos[1]] = 1.0 - g
    w = [pack_weight(m, "e2m1") for m in n((E + 1, N, K)) / np.sqrt(N) / s[None]]
    return {
        "dyT": (n((N, T)) * s).astype(np.float32),
        "w_words": np.stack([m[0] for m in w]),
        "w_scales": np.stack([m[1] for m in w]),
        "gate": np.tile(w_slot, (N, 1)).astype(np.float32),
        "offs": striped(slot_token),
        "pos1": striped(pos[0]),
        "pos2": striped(pos[1]),
    }


def reference(dyT, w_words, w_scales, gate, offs, pos1, pos2):
    idx = unstriped(offs)
    w = np.stack([unpack_weight(w_words[e], w_scales[e], "e2m1") for e in range(E + 1)])
    gq = mxq(f64(gate) * f64(dyT)[:, idx], 0, "e5m2")
    wq = w
    ds = wq[E].T @ mxq(f64(dyT), 0, "e5m2")
    dx = by_expert(wq, gq)
    return ds + dx[:, unstriped(pos1)] + dx[:, unstriped(pos2)]

@@ -1,0 +1,210 @@
+from contextlib import ExitStack
+
+import concourse.mybir as mybir
+from concourse.masks import make_identity
+
+K, T, E, C, N = 128, 2048, 8, 512, 512
+S = E * C
+FLOPS = 2 * N * K * (S + T)
+BYTES = 4 * N * T + 4 * S + (E + 1) * (128 * 256 + 16 * 128) + 2 * (S + 2 * T) + 4 * K * T
+
+F32 = mybir.dt.float32
+BF16 = mybir.dt.bfloat16
+I32 = mybir.dt.int32
+U32 = mybir.dt.uint32
+U16 = mybir.dt.uint16
+U8 = mybir.dt.uint8
+E5M2 = mybir.dt.float8_e5m2_x4
+E2M1 = mybir.dt.float4_e2m1fn_x4
+MULT = mybir.AluOpType.mult
+ADD = mybir.AluOpType.add
+
+P = 128
+PACK = 4
+LINE = 4
+PER_COL = 16
+CHUNKS = (1536, 1024, 512, 512, 256, 256)
+FIRST_PIECE = 512
+SHARED_PIECE = 256
+GROUP = 512
+
+
+def tile_moe_bds_lin_none_kernel(tc, dyT, w_words, w_scales, gate, offs, pos1, pos2, out):
+    nc = tc.nc
+    with ExitStack() as ctx:
+        keep = ctx.enter_context(tc.tile_pool(name="keep", bufs=1))
+        psum = ctx.enter_context(tc.psum_pool(name="psum", bufs=1))
+
+        starts = [sum(CHUNKS[:i]) for i in range(len(CHUNKS))]
+        dy_rows = dyT.rearrange("(p t) c -> p t c", t=PACK)
+
+        planes = [keep.tile([P, T], F32, name=f"plane{t}", tag=f"plane{t}", align_bytes=64) for t in range(PACK)]
+        offs_sb = keep.tile([P, S // PER_COL], U16, name="offs_sb")
+        pos1_sb = keep.tile([P, T // PER_COL], U16, name="pos1_sb")
+        pos2_sb = keep.tile([P, T // PER_COL], U16, name="pos2_sb")
+        gate_sb = keep.tile([P, S], F32, name="gate_sb")
+        n_shared = T // SHARED_PIECE
+        dy_shared = [keep.tile([P, PACK, SHARED_PIECE], F32, name=f"dy_shared{i}", tag=f"stage{i}") for i in range(n_shared)]
+        w_codes = keep.tile([P, E + 1, 2 * K], U8, name="w_codes", align_bytes=64)
+        w_plane = keep.tile([P, E + 1, K], U8, name="w_plane", align_bytes=64)
+        ident = keep.tile([P, P], F32, name="ident")
+
+        nc.vector.memset(w_plane[:].bitcast(I32), 0)
+        make_identity(nc, ident[:])
+
+        def load_gate(lo, hi):
+            nc.sync.dma_start(out=gate_sb[:, lo:hi], in_=gate[0:P, lo:hi])
+
+        def load_shared(i):
+            nc.sync.dma_start(out=dy_shared[i][:], in_=dy_rows[:, :, i * SHARED_PIECE : (i + 1) * SHARED_PIECE])
+
+        nc.sync.dma_start(out=planes[0][:], in_=dy_rows[:, 0, :])
+        nc.sync.dma_start(offs_sb[:], offs)
+        load_gate(0, FIRST_PIECE)
+        load_gate(FIRST_PIECE, CHUNKS[0])
+        nc.sync.dma_start(out=planes[1][:], in_=dy_rows[:, 1, :])
+        load_shared(0)
+        nc.sync.dma_start(out=planes[2][:], in_=dy_rows[:, 2, :])
+        load_shared(1)
+        nc.sync.dma_start(out=planes[3][:], in_=dy_rows[:, 3, :])
+        load_shared(2)
+        load_gate(starts[1], starts[2])
+        load_shared(3)
+        nc.sync.dma_start(out=w_codes[:].bitcast(I32), in_=w_words.rearrange("e a p b -> p (e a) b").bitcast(I32))
+        scale_rows = w_scales.rearrange("e a f k -> f (e a) k").bitcast(I32)
+        for r in range(4):
+            nc.sync.dma_start(out=w_plane[r:P:32].bitcast(I32), in_=scale_rows[r:16:4])
+        load_gate(starts[2], S)
+        for i in range(4, n_shared):
+            load_shared(i)
+        nc.sync.dma_start(pos1_sb[:], pos1)
+        nc.sync.dma_start(pos2_sb[:], pos2)
+
+        g_f32 = [keep.tile([P, PACK, n], F32, name=f"g_f32_{i}", tag=f"g_f32_{i % 3}") for i, n in enumerate(CHUNKS)]
+        g_bf = [keep.tile([P, C, PACK], BF16, name=f"g_bf{e}", tag="g_bf", bufs=3, align_bytes=64) for e in range(E - 1)]
+        g_bf.append(keep.tile([P, C, PACK], BF16, name="g_bf_last", tag="last", align_bytes=64))
+        g_codes = [keep.tile([P, C], U32, name=f"g_codes{e}", tag="g_codes", bufs=3, align_bytes=64) for e in range(E)]
+        g_plane = [keep.tile([P, C], U8, name=f"g_plane{e}", align_bytes=64) for e in range(E)]
+        dx = keep.tile([P, S], F32, name="dx")
+
+        def gather_g(i, t, lo, hi):
+            a, b = starts[i] + lo, starts[i] + hi
+            nc.vector.tensor_tensor(
+                g_f32[i][:, t, lo:hi], planes[t][:].indirect(offs_sb[:, a // PER_COL : b // PER_COL]), gate_sb[:, a:b], MULT
+            )
+
+        def interleave(dst, src):
+            nc.scalar.copy(
+                out=dst.rearrange("p (c i) t -> p c t i", i=LINE), in_=src.rearrange("p t (c i) -> p c t i", i=LINE)
+            )
+
+        def quantize(codes, plane, values):
+            nc.vector.quantize_mx(out=codes.bitcast(E5M2), scales=plane, in_=values.rearrange("p c t -> p (c t)"))
+
+        def multiply(e, codes, plane, dst):
+            acc = psum.tile([P, C], F32, name="acc", tag="acc", bufs=2)
+            nc.tensor.matmul_mx(
+                out=acc[:],
+                lhsT=w_codes[:, e, :].bitcast(E2M1),
+                lhsT_scale=w_plane[:, e, :],
+                rhs=codes.bitcast(E5M2),
+                rhs_scale=plane[:],
+                start=True,
+                stop=True,
+            )
+            nc.scalar.copy(out=dst, in_=acc[:])
+
+        def pieces(i):
+            end = starts[i] + CHUNKS[i]
+            return [(lo, min(end, lo + C)) for lo in range(starts[i], end, C)]
+
+        def finish_chunk(i):
+            for lo, hi in chunk_pieces[i]:
+                e = lo // C
+                cols = slice(lo - e * C, hi - e * C)
+                quantize(g_codes[e][:, cols], g_plane[e][:, cols], g_bf[e][:, cols, :])
+                if hi % C == 0:
+                    multiply(e, g_codes[e][:], g_plane[e], dx[:, e * C : (e + 1) * C])
+
+        chunk_pieces = [pieces(i) for i in range(len(CHUNKS))]
+
+        n_groups = T // GROUP
+        s_bf = [keep.tile([P, GROUP, PACK], BF16, name=f"s_bf{q}", align_bytes=64) for q in range(n_groups)]
+        per_group = GROUP // SHARED_PIECE
+        for i in range(n_shared):
+            h = i % per_group
+            interleave(s_bf[i // per_group][:, h * SHARED_PIECE : (h + 1) * SHARED_PIECE, :], dy_shared[i][:])
+
+        for i, n in enumerate(CHUNKS):
+            for t in range(PACK):
+                if i == 0 and t == 0:
+                    gather_g(i, t, 0, FIRST_PIECE)
+                    gather_g(i, t, FIRST_PIECE, n)
+                else:
+                    gather_g(i, t, 0, n)
+            for lo, hi in chunk_pieces[i]:
+                e = lo // C
+                interleave(g_bf[e][:, lo - e * C : hi - e * C, :], g_f32[i][:, :, lo - starts[i] : hi - starts[i]])
+            if i > 0:
+                finish_chunk(i - 1)
+        finish_chunk(len(CHUNKS) - 1)
+
+        s_codes = [keep.tile([P, GROUP], U32, name=f"s_codes{q}", tag=f"plane{q}", align_bytes=64)[:] for q in range(2)]
+        s_late = keep.tile([P, 2 * GROUP], U32, name="s_late", tag="last", align_bytes=64)
+        s_codes += [s_late[:, 0:GROUP], s_late[:, GROUP : 2 * GROUP]]
+        s_plane = [keep.tile([P, GROUP], U8, name=f"s_plane{q}", align_bytes=64) for q in range(n_groups)]
+        ds = [keep.tile([P, GROUP], F32, name=f"ds{q}") for q in range(n_groups)]
+        for q in range(n_groups):
+            for h in range(per_group):
+                cols = slice(h * SHARED_PIECE, (h + 1) * SHARED_PIECE)
+                quantize(s_codes[q][:, cols], s_plane[q][:, cols], s_bf[q][:, cols, :])
+            multiply(E, s_codes[q], s_plane[q], ds[q][:])
+
+        first = keep.tile([P, T], F32, name="first", tag="plane3", align_bytes=64)
+        second = [keep.tile([P, GROUP], F32, name=f"second{q}") for q in range(n_groups)]
+        turned = [psum.tile([P, GROUP], F32, name=f"turned{q}") for q in range(n_groups)]
+        blocks = GROUP // P
+
+        def turn(bank, src, start, stop):
+            for j in range(blocks):
+                nc.tensor.matmul(
+                    bank[:, j * P : (j + 1) * P],
+                    src[:, j * P : (j + 1) * P],
+                    ident[:],
+                    start=start and j == 0,
+                    stop=stop and j == blocks - 1,
+                    is_transpose=True,
+                )
+
+        def turn_back(q, bank):
+            sums = keep.tile([P, GROUP], F32, name=f"sums{q}", tag=f"stage{q}")
+            nc.scalar.copy(out=sums[:], in_=turned[q][:])
+            for j in range(blocks):
+                nc.tensor.transpose(bank[:, j * P : (j + 1) * P], sums[:, j * P : (j + 1) * P], ident[:])
+
+        on_tensor = 2
+        for q in range(n_groups):
+            turn(turned[q], ds[q], True, False)
+        half = T // 2
+        for h in range(2):
+            nc.vector.tensor_copy(
+                first[:, h * half : (h + 1) * half],
+                dx[:].indirect(pos1_sb[:, h * half // PER_COL : (h + 1) * half // PER_COL]),
+            )
+        for q in range(n_groups):
+            nc.vector.tensor_copy(second[q][:], dx[:].indirect(pos2_sb[:, q * GROUP // PER_COL : (q + 1) * GROUP // PER_COL]))
+        for q in range(n_groups):
+            turn(turned[q], first[:, q * GROUP : (q + 1) * GROUP], False, q >= on_tensor)
+        held = [psum.tile([P, GROUP], F32, name=f"held{q}") for q in range(on_tensor, n_groups)]
+        for q in range(on_tensor, n_groups):
+            turn_back(q, held[q - on_tensor])
+        for q in range(n_groups):
+            result = keep.tile([P, GROUP], F32, name=f"result{q}", tag=f"stage{n_groups + q}")
+            if q < on_tensor:
+                turn(turned[q], second[q], False, True)
+                back = psum.tile([P, C], F32, name="back", tag="acc", bufs=2)
+                turn_back(q, back)
+                nc.scalar.copy(out=result[:], in_=back[:])
+            else:
+                nc.vector.tensor_tensor(result[:], held[q - on_tensor][:], second[q][:], ADD)
+            nc.sync.dma_start(out=out[:, q * GROUP : (q + 1) * GROUP], in_=result[:])

@@ -23,10 +23,11 @@ P = 128
 PACK = 4
 LINE = 4
 PER_COL = 16
-CHUNKS = (1536, 1024, 512, 512, 256, 256)
+CHUNKS = (1536, 1024, 768, 512, 256)
 FIRST_PIECE = 512
 SHARED_PIECE = 256
 GROUP = 512
+QUANTS = ((0, 1024, 1, 3), (1024, 2048, 2, 3), (2048, 3072, 3, 3), (3072, 3584, 4, 3), (3584, 3840, 4, 3), (3840, 4096, 4, 3))
 
 
 def tile_moe_bds_lin_none_kernel(tc, dyT, w_words, w_scales, gate, offs, pos1, pos2, out):
@@ -35,7 +36,7 @@ def tile_moe_bds_lin_none_kernel(tc, dyT, w_words, w_scales, gate, offs, pos1, p
         keep = ctx.enter_context(tc.tile_pool(name="keep", bufs=1))
         psum = ctx.enter_context(tc.psum_pool(name="psum", bufs=1))
 
-        starts = [sum(CHUNKS[:i]) for i in range(len(CHUNKS))]
+        starts = [sum(CHUNKS[:i]) for i in range(len(CHUNKS) + 1)]
         dy_rows = dyT.rearrange("(p t) c -> p t c", t=PACK)
 
         planes = [keep.tile([P, T], F32, name=f"plane{t}", tag=f"plane{t}", align_bytes=64) for t in range(PACK)]
@@ -52,40 +53,57 @@ def tile_moe_bds_lin_none_kernel(tc, dyT, w_words, w_scales, gate, offs, pos1, p
         nc.vector.memset(w_plane[:].bitcast(I32), 0)
         make_identity(nc, ident[:])
 
+        def load_plane(t):
+            nc.sync.dma_start(out=planes[t][:], in_=dy_rows[:, t, :])
+
         def load_gate(lo, hi):
             nc.sync.dma_start(out=gate_sb[:, lo:hi], in_=gate[0:P, lo:hi])
 
         def load_shared(i):
             nc.sync.dma_start(out=dy_shared[i][:], in_=dy_rows[:, :, i * SHARED_PIECE : (i + 1) * SHARED_PIECE])
 
-        nc.sync.dma_start(out=planes[0][:], in_=dy_rows[:, 0, :])
+        def load_weights():
+            nc.sync.dma_start(out=w_codes[:].bitcast(I32), in_=w_words.rearrange("e a p b -> p (e a) b").bitcast(I32))
+            scale_rows = w_scales.rearrange("e a f k -> f (e a) k").bitcast(I32)
+            for r in range(4):
+                nc.sync.dma_start(out=w_plane[r:P:32].bitcast(I32), in_=scale_rows[r:16:4])
+
+        load_plane(0)
         nc.sync.dma_start(offs_sb[:], offs)
         load_gate(0, FIRST_PIECE)
         load_gate(FIRST_PIECE, CHUNKS[0])
-        nc.sync.dma_start(out=planes[1][:], in_=dy_rows[:, 1, :])
+        load_plane(1)
         load_shared(0)
-        nc.sync.dma_start(out=planes[2][:], in_=dy_rows[:, 2, :])
+        load_plane(2)
         load_shared(1)
-        nc.sync.dma_start(out=planes[3][:], in_=dy_rows[:, 3, :])
+        load_plane(3)
         load_shared(2)
         load_gate(starts[1], starts[2])
-        load_shared(3)
-        nc.sync.dma_start(out=w_codes[:].bitcast(I32), in_=w_words.rearrange("e a p b -> p (e a) b").bitcast(I32))
-        scale_rows = w_scales.rearrange("e a f k -> f (e a) k").bitcast(I32)
-        for r in range(4):
-            nc.sync.dma_start(out=w_plane[r:P:32].bitcast(I32), in_=scale_rows[r:16:4])
+        for i in range(3, 6):
+            load_shared(i)
+        load_weights()
         load_gate(starts[2], S)
-        for i in range(4, n_shared):
+        for i in range(6, n_shared):
             load_shared(i)
         nc.sync.dma_start(pos1_sb[:], pos1)
         nc.sync.dma_start(pos2_sb[:], pos2)
 
-        g_f32 = [keep.tile([P, PACK, n], F32, name=f"g_f32_{i}", tag=f"g_f32_{i % 3}") for i, n in enumerate(CHUNKS)]
-        g_bf = [keep.tile([P, C, PACK], BF16, name=f"g_bf{e}", tag="g_bf", bufs=3, align_bytes=64) for e in range(E - 1)]
-        g_bf.append(keep.tile([P, C, PACK], BF16, name="g_bf_last", tag="last", align_bytes=64))
-        g_codes = [keep.tile([P, C], U32, name=f"g_codes{e}", tag="g_codes", bufs=3, align_bytes=64) for e in range(E)]
-        g_plane = [keep.tile([P, C], U8, name=f"g_plane{e}", align_bytes=64) for e in range(E)]
+        last = (E - 1) * C
+        g_f32 = [keep.tile([P, PACK, n], F32, name=f"g_f32_{i}", tag=f"g_f32_{i}" if i < 2 else f"pair{i - 2}", align_bytes=64) for i, n in enumerate(CHUNKS)]
+        g_bf_pairs = [keep.tile([P, 2 * C, PACK], BF16, name=f"g_bf_pair{u}", tag=f"pair{u}", align_bytes=64) for u in range(3)]
+        g_bf_pairs.append(keep.tile([P, C, PACK], BF16, name="g_bf_6", align_bytes=64))
+        g_bf_last = keep.tile([P, C, PACK], BF16, name="g_bf_last", tag="after_last_quantize", align_bytes=64)
+        g_codes_main = keep.tile([P, last], U32, name="g_codes_main", align_bytes=64)
+        g_codes_last = keep.tile([P, C], U32, name="g_codes_last", tag="after_last_product", align_bytes=64)
+        g_plane = keep.tile([P, S], U8, name="g_plane", align_bytes=64)
         dx = keep.tile([P, S], F32, name="dx")
+
+        def g_bf(lo, hi):
+            base = lo // (2 * C) * 2 * C
+            return g_bf_pairs[lo // (2 * C)][:, lo - base : hi - base, :] if lo < last else g_bf_last[:, lo - last : hi - last, :]
+
+        def g_codes(lo, hi):
+            return g_codes_main[:, lo:hi] if lo < last else g_codes_last[:, lo - last : hi - last]
 
         def gather_g(i, t, lo, hi):
             a, b = starts[i] + lo, starts[i] + hi
@@ -101,39 +119,34 @@ def tile_moe_bds_lin_none_kernel(tc, dyT, w_words, w_scales, gate, offs, pos1, p
         def quantize(codes, plane, values):
             nc.vector.quantize_mx(out=codes.bitcast(E5M2), scales=plane, in_=values.rearrange("p c t -> p (c t)"))
 
-        def multiply(e, codes, plane, dst):
-            acc = psum.tile([P, C], F32, name="acc", tag="acc", bufs=2)
+        def multiply(e, codes, plane, acc):
             nc.tensor.matmul_mx(
                 out=acc[:],
                 lhsT=w_codes[:, e, :].bitcast(E2M1),
                 lhsT_scale=w_plane[:, e, :],
                 rhs=codes.bitcast(E5M2),
-                rhs_scale=plane[:],
+                rhs_scale=plane,
                 start=True,
                 stop=True,
             )
+
+        def multiply_into(e, codes, plane, dst):
+            acc = psum.tile([P, C], F32, name="acc", tag="acc", bufs=2)
+            multiply(e, codes, plane, acc)
             nc.scalar.copy(out=dst, in_=acc[:])
 
-        def pieces(i):
-            end = starts[i] + CHUNKS[i]
-            return [(lo, min(end, lo + C)) for lo in range(starts[i], end, C)]
-
-        def finish_chunk(i):
-            for lo, hi in chunk_pieces[i]:
-                e = lo // C
-                cols = slice(lo - e * C, hi - e * C)
-                quantize(g_codes[e][:, cols], g_plane[e][:, cols], g_bf[e][:, cols, :])
-                if hi % C == 0:
-                    multiply(e, g_codes[e][:], g_plane[e], dx[:, e * C : (e + 1) * C])
-
-        chunk_pieces = [pieces(i) for i in range(len(CHUNKS))]
+        def quantize_slots(lo, hi):
+            quantize(g_codes(lo, hi), g_plane[:, lo:hi], g_bf(lo, hi))
+            for e in range(lo // C, hi // C):
+                cols = slice(e * C, (e + 1) * C)
+                multiply_into(e, g_codes(cols.start, cols.stop), g_plane[:, cols], dx[:, cols])
 
         n_groups = T // GROUP
-        s_bf = [keep.tile([P, GROUP, PACK], BF16, name=f"s_bf{q}", align_bytes=64) for q in range(n_groups)]
+        tail = n_groups - 1
         per_group = GROUP // SHARED_PIECE
-        for i in range(n_shared):
-            h = i % per_group
-            interleave(s_bf[i // per_group][:, h * SHARED_PIECE : (h + 1) * SHARED_PIECE, :], dy_shared[i][:])
+        s_bf_early = keep.tile([P, tail * GROUP, PACK], BF16, name="s_bf_early", align_bytes=64)
+        for i in range(tail * per_group):
+            interleave(s_bf_early[:, i * SHARED_PIECE : (i + 1) * SHARED_PIECE, :], dy_shared[i][:])
 
         for i, n in enumerate(CHUNKS):
             for t in range(PACK):
@@ -142,28 +155,38 @@ def tile_moe_bds_lin_none_kernel(tc, dyT, w_words, w_scales, gate, offs, pos1, p
                     gather_g(i, t, FIRST_PIECE, n)
                 else:
                     gather_g(i, t, 0, n)
-            for lo, hi in chunk_pieces[i]:
-                e = lo // C
-                interleave(g_bf[e][:, lo - e * C : hi - e * C, :], g_f32[i][:, :, lo - starts[i] : hi - starts[i]])
-            if i > 0:
-                finish_chunk(i - 1)
-        finish_chunk(len(CHUNKS) - 1)
+                if t == PACK - 1:
+                    cuts = sorted({starts[i], starts[i + 1], *range(-(-starts[i] // C) * C, starts[i + 1], C)})
+                    for lo, hi in zip(cuts, cuts[1:]):
+                        interleave(g_bf(lo, hi), g_f32[i][:, :, lo - starts[i] : hi - starts[i]])
+                for lo, hi, chunk, plane in QUANTS:
+                    if (chunk, plane) == (i, t):
+                        quantize_slots(lo, hi)
 
-        s_codes = [keep.tile([P, GROUP], U32, name=f"s_codes{q}", tag=f"plane{q}", align_bytes=64)[:] for q in range(2)]
-        s_late = keep.tile([P, 2 * GROUP], U32, name="s_late", tag="last", align_bytes=64)
-        s_codes += [s_late[:, 0:GROUP], s_late[:, GROUP : 2 * GROUP]]
-        s_plane = [keep.tile([P, GROUP], U8, name=f"s_plane{q}", align_bytes=64) for q in range(n_groups)]
-        ds = [keep.tile([P, GROUP], F32, name=f"ds{q}") for q in range(n_groups)]
-        for q in range(n_groups):
-            for h in range(per_group):
-                cols = slice(h * SHARED_PIECE, (h + 1) * SHARED_PIECE)
-                quantize(s_codes[q][:, cols], s_plane[q][:, cols], s_bf[q][:, cols, :])
-            multiply(E, s_codes[q], s_plane[q], ds[q][:])
+        s_plane = keep.tile([P, T], U8, name="s_plane", align_bytes=64)
+        s_codes_0 = keep.tile([P, GROUP], U32, name="s_codes_0", tag="plane2", align_bytes=64)
+        s_codes_12 = keep.tile([P, 2 * GROUP], U32, name="s_codes_12", tag="after_last_quantize", align_bytes=64)
+        s_codes_3 = keep.tile([P, GROUP], U32, name="s_codes_3", tag="plane1", align_bytes=64)
+        quantize(s_codes_0[:], s_plane[:, 0:GROUP], s_bf_early[:, 0:GROUP, :])
+        quantize(s_codes_12[:], s_plane[:, GROUP : tail * GROUP], s_bf_early[:, GROUP : tail * GROUP, :])
+        s_codes = [s_codes_0[:], s_codes_12[:, 0:GROUP], s_codes_12[:, GROUP : 2 * GROUP]]
+        ds_all = keep.tile([P, tail * GROUP], F32, name="ds_all", tag="after_ds")
+        ds = [ds_all[:, q * GROUP : (q + 1) * GROUP] for q in range(tail)]
+        for q in range(tail):
+            multiply_into(E, s_codes[q], s_plane[:, q * GROUP : (q + 1) * GROUP], ds[q])
+        s_bf_tail = keep.tile([P, GROUP, PACK], BF16, name="s_bf_tail", tag="after_last_product", align_bytes=64)
+        for h in range(per_group):
+            interleave(s_bf_tail[:, h * SHARED_PIECE : (h + 1) * SHARED_PIECE, :], dy_shared[tail * per_group + h][:])
 
-        first = keep.tile([P, T], F32, name="first", tag="plane3", align_bytes=64)
-        second = [keep.tile([P, GROUP], F32, name=f"second{q}") for q in range(n_groups)]
-        turned = [psum.tile([P, GROUP], F32, name=f"turned{q}") for q in range(n_groups)]
+        head = tail * GROUP
+        first = keep.tile([P, head], F32, name="first", tag="plane3", align_bytes=64)
+        second = keep.tile([P, head], F32, name="second", tag="after_ds")
+        tail_pair = keep.tile([P, 2, GROUP], F32, name="tail_pair", tag="after_last_product", align_bytes=64)
+        turned = [psum.tile([P, GROUP], F32, name=f"turned{q}") for q in range(tail)]
         blocks = GROUP // P
+
+        def gather_dx(dst, pos_sb, lo, hi):
+            nc.vector.tensor_copy(dst, dx[:].indirect(pos_sb[:, lo // PER_COL : hi // PER_COL]))
 
         def turn(bank, src, start, stop):
             for j in range(blocks):
@@ -176,35 +199,42 @@ def tile_moe_bds_lin_none_kernel(tc, dyT, w_words, w_scales, gate, offs, pos1, p
                     is_transpose=True,
                 )
 
-        def turn_back(q, bank):
-            sums = keep.tile([P, GROUP], F32, name=f"sums{q}", tag=f"stage{q}")
-            nc.scalar.copy(out=sums[:], in_=turned[q][:])
-            for j in range(blocks):
-                nc.tensor.transpose(bank[:, j * P : (j + 1) * P], sums[:, j * P : (j + 1) * P], ident[:])
-
-        on_tensor = 2
-        for q in range(n_groups):
+        for q in range(tail):
             turn(turned[q], ds[q], True, False)
-        half = T // 2
+        gather_dx(first[:], pos1_sb, 0, head)
+        for q in range(tail):
+            turn(turned[q], first[:, q * GROUP : (q + 1) * GROUP], False, False)
+        for q in range(tail):
+            gather_dx(second[:, q * GROUP : (q + 1) * GROUP], pos2_sb, q * GROUP, (q + 1) * GROUP)
+        tail_cols = slice(head, T)
+        quantize(s_codes_3[:], s_plane[:, tail_cols], s_bf_tail[:])
+        ds_tail = psum.tile([P, GROUP], F32, name="ds_tail")
+        multiply(E, s_codes_3[:], s_plane[:, tail_cols], ds_tail)
+        gather_dx(tail_pair[:, 0, :], pos1_sb, head, T)
+        gather_dx(tail_pair[:, 1, :], pos2_sb, head, T)
+        sums = [keep.tile([P, GROUP], F32, name=f"sums{q}", tag=f"stage{q}") for q in range(tail)]
+        backs = {}
+        for step in range(tail + 1):
+            q = step - 1
+            if step < tail:
+                turn(turned[step], second[:, step * GROUP : (step + 1) * GROUP], False, True)
+            if q >= 0:
+                backs[q] = psum.tile([P, GROUP], F32, name="back", tag="back", bufs=2)
+                for j in range(blocks):
+                    nc.tensor.transpose(backs[q][:, j * P : (j + 1) * P], sums[q][:, j * P : (j + 1) * P], ident[:])
+            if step < tail:
+                nc.scalar.copy(out=sums[step][:], in_=turned[step][:])
+            if q >= 0:
+                result = keep.tile([P, GROUP], F32, name=f"result{q}", tag=f"stage{tail + q}")
+                nc.scalar.copy(out=result[:], in_=backs[q][:])
+                nc.sync.dma_start(out=out[:, q * GROUP : (q + 1) * GROUP], in_=result[:])
+        half = GROUP // 2
+        partial = keep.tile([P, GROUP], F32, name="partial", tag="g_f32_0", align_bytes=64)
+        result = keep.tile([P, GROUP], F32, name="result_tail", tag="g_f32_1", align_bytes=64)
         for h in range(2):
-            nc.vector.tensor_copy(
-                first[:, h * half : (h + 1) * half],
-                dx[:].indirect(pos1_sb[:, h * half // PER_COL : (h + 1) * half // PER_COL]),
-            )
-        for q in range(n_groups):
-            nc.vector.tensor_copy(second[q][:], dx[:].indirect(pos2_sb[:, q * GROUP // PER_COL : (q + 1) * GROUP // PER_COL]))
-        for q in range(n_groups):
-            turn(turned[q], first[:, q * GROUP : (q + 1) * GROUP], False, q >= on_tensor)
-        held = [psum.tile([P, GROUP], F32, name=f"held{q}") for q in range(on_tensor, n_groups)]
-        for q in range(on_tensor, n_groups):
-            turn_back(q, held[q - on_tensor])
-        for q in range(n_groups):
-            result = keep.tile([P, GROUP], F32, name=f"result{q}", tag=f"stage{n_groups + q}")
-            if q < on_tensor:
-                turn(turned[q], second[q], False, True)
-                back = psum.tile([P, C], F32, name="back", tag="acc", bufs=2)
-                turn_back(q, back)
-                nc.scalar.copy(out=result[:], in_=back[:])
-            else:
-                nc.vector.tensor_tensor(result[:], held[q - on_tensor][:], second[q][:], ADD)
-            nc.sync.dma_start(out=out[:, q * GROUP : (q + 1) * GROUP], in_=result[:])
+            cols = slice(h * half, (h + 1) * half)
+            nc.vector.tensor_tensor(partial[:, cols], ds_tail[:, cols], tail_pair[:, 0, cols], ADD)
+        for h in range(2):
+            cols = slice(h * half, (h + 1) * half)
+            nc.vector.tensor_tensor(result[:, cols], partial[:, cols], tail_pair[:, 1, cols], ADD)
+            nc.sync.dma_start(out=out[:, tail_cols][:, cols], in_=result[:, cols])

@@ -24,7 +24,7 @@ PACK = 4
 LINE = 4
 PER_COL = 16
 CHUNKS = (1536, 1024, 768, 512, 256)
-FIRST_PIECE = 512
+FIRST_CUTS = (0, 256, 768, 1536)
 SHARED_PIECE = 256
 GROUP = 512
 QUANTS = ((0, 1024, 1, 3), (1024, 2048, 2, 3), (2048, 3072, 3, 3), (3072, 3584, 4, 3), (3584, 3840, 4, 3), (3840, 4096, 4, 3))
@@ -70,16 +70,16 @@ def tile_moe_bds_lin_none_kernel(tc, dyT, w_words, w_scales, gate, offs, pos1, p
 
         load_plane(0)
         nc.sync.dma_start(offs_sb[:], offs)
-        load_gate(0, FIRST_PIECE)
-        load_gate(FIRST_PIECE, CHUNKS[0])
+        for lo, hi in zip(FIRST_CUTS, FIRST_CUTS[1:]):
+            load_gate(lo, hi)
         load_plane(1)
-        load_shared(0)
         load_plane(2)
-        load_shared(1)
+        load_shared(0)
         load_plane(3)
-        load_shared(2)
+        for i in range(1, 4):
+            load_shared(i)
         load_gate(starts[1], starts[2])
-        for i in range(3, 6):
+        for i in range(4, 6):
             load_shared(i)
         load_weights()
         load_gate(starts[2], S)
@@ -151,8 +151,8 @@ def tile_moe_bds_lin_none_kernel(tc, dyT, w_words, w_scales, gate, offs, pos1, p
         for i, n in enumerate(CHUNKS):
             for t in range(PACK):
                 if i == 0 and t == 0:
-                    gather_g(i, t, 0, FIRST_PIECE)
-                    gather_g(i, t, FIRST_PIECE, n)
+                    for lo, hi in zip(FIRST_CUTS, FIRST_CUTS[1:]):
+                        gather_g(i, t, lo, hi)
                 else:
                     gather_g(i, t, 0, n)
                 if t == PACK - 1:
@@ -170,8 +170,7 @@ def tile_moe_bds_lin_none_kernel(tc, dyT, w_words, w_scales, gate, offs, pos1, p
         quantize(s_codes_0[:], s_plane[:, 0:GROUP], s_bf_early[:, 0:GROUP, :])
         quantize(s_codes_12[:], s_plane[:, GROUP : tail * GROUP], s_bf_early[:, GROUP : tail * GROUP, :])
         s_codes = [s_codes_0[:], s_codes_12[:, 0:GROUP], s_codes_12[:, GROUP : 2 * GROUP]]
-        ds_all = keep.tile([P, tail * GROUP], F32, name="ds_all", tag="after_ds")
-        ds = [ds_all[:, q * GROUP : (q + 1) * GROUP] for q in range(tail)]
+        ds = [keep.tile([P, GROUP], F32, name=f"ds{q}", tag=f"after_ds{q}")[:] for q in range(tail)]
         for q in range(tail):
             multiply_into(E, s_codes[q], s_plane[:, q * GROUP : (q + 1) * GROUP], ds[q])
         s_bf_tail = keep.tile([P, GROUP, PACK], BF16, name="s_bf_tail", tag="after_last_product", align_bytes=64)
@@ -180,7 +179,9 @@ def tile_moe_bds_lin_none_kernel(tc, dyT, w_words, w_scales, gate, offs, pos1, p
 
         head = tail * GROUP
         first = keep.tile([P, head], F32, name="first", tag="plane3", align_bytes=64)
-        second = keep.tile([P, head], F32, name="second", tag="after_ds")
+        second_0 = keep.tile([P, GROUP], F32, name="second_0", tag="after_ds1")
+        second_12 = keep.tile([P, 2, GROUP], F32, name="second_12", tag="after_ds2")
+        second = [second_0[:], second_12[:, 0, :], second_12[:, 1, :]]
         tail_pair = keep.tile([P, 2, GROUP], F32, name="tail_pair", tag="after_last_product", align_bytes=64)
         turned = [psum.tile([P, GROUP], F32, name=f"turned{q}") for q in range(tail)]
         blocks = GROUP // P
@@ -201,11 +202,11 @@ def tile_moe_bds_lin_none_kernel(tc, dyT, w_words, w_scales, gate, offs, pos1, p
 
         for q in range(tail):
             turn(turned[q], ds[q], True, False)
-        gather_dx(first[:], pos1_sb, 0, head)
         for q in range(tail):
+            gather_dx(first[:, q * GROUP : (q + 1) * GROUP], pos1_sb, q * GROUP, (q + 1) * GROUP)
             turn(turned[q], first[:, q * GROUP : (q + 1) * GROUP], False, False)
         for q in range(tail):
-            gather_dx(second[:, q * GROUP : (q + 1) * GROUP], pos2_sb, q * GROUP, (q + 1) * GROUP)
+            gather_dx(second[q], pos2_sb, q * GROUP, (q + 1) * GROUP)
         tail_cols = slice(head, T)
         quantize(s_codes_3[:], s_plane[:, tail_cols], s_bf_tail[:])
         ds_tail = psum.tile([P, GROUP], F32, name="ds_tail")
@@ -217,7 +218,7 @@ def tile_moe_bds_lin_none_kernel(tc, dyT, w_words, w_scales, gate, offs, pos1, p
         for step in range(tail + 1):
             q = step - 1
             if step < tail:
-                turn(turned[step], second[:, step * GROUP : (step + 1) * GROUP], False, True)
+                turn(turned[step], second[step], False, True)
             if q >= 0:
                 backs[q] = psum.tile([P, GROUP], F32, name="back", tag="back", bufs=2)
                 for j in range(blocks):

from contextlib import ExitStack

import concourse.mybir as mybir
from concourse.masks import make_identity

K, T, E, C, N = 128, 2048, 8, 512, 512
S = E * C
FLOPS = 2 * N * K * (S + T)
BYTES = 4 * N * T + 4 * S + (E + 1) * (128 * 256 + 16 * 128) + 2 * (S + 2 * T) + 4 * K * T

F32 = mybir.dt.float32
BF16 = mybir.dt.bfloat16
I32 = mybir.dt.int32
U32 = mybir.dt.uint32
U16 = mybir.dt.uint16
U8 = mybir.dt.uint8
E5M2 = mybir.dt.float8_e5m2_x4
E2M1 = mybir.dt.float4_e2m1fn_x4
MULT = mybir.AluOpType.mult
ADD = mybir.AluOpType.add

P = 128
PACK = 4
LINE = 4
PER_COL = 16
CHUNKS = (1536, 1024, 768, 512, 256)
FIRST_CUTS = (0, 256, 768, 1536)
SHARED_PIECE = 256
GROUP = 512
QUANTS = ((0, 1024, 1, 3), (1024, 2048, 2, 3), (2048, 3072, 3, 3), (3072, 3584, 4, 3), (3584, 3840, 4, 3), (3840, 4096, 4, 3))


def tile_moe_bds_lin_none_kernel(tc, dyT, w_words, w_scales, gate, offs, pos1, pos2, out):
    nc = tc.nc
    with ExitStack() as ctx:
        keep = ctx.enter_context(tc.tile_pool(name="keep", bufs=1))
        psum = ctx.enter_context(tc.psum_pool(name="psum", bufs=1))

        starts = [sum(CHUNKS[:i]) for i in range(len(CHUNKS) + 1)]
        dy_rows = dyT.rearrange("(p t) c -> p t c", t=PACK)

        planes = [keep.tile([P, T], F32, name=f"plane{t}", tag=f"plane{t}", align_bytes=64) for t in range(PACK)]
        offs_sb = keep.tile([P, S // PER_COL], U16, name="offs_sb")
        pos1_sb = keep.tile([P, T // PER_COL], U16, name="pos1_sb")
        pos2_sb = keep.tile([P, T // PER_COL], U16, name="pos2_sb")
        gate_sb = keep.tile([P, S], F32, name="gate_sb")
        n_shared = T // SHARED_PIECE
        dy_shared = [keep.tile([P, PACK, SHARED_PIECE], F32, name=f"dy_shared{i}", tag=f"stage{i}") for i in range(n_shared)]
        w_codes = keep.tile([P, E + 1, 2 * K], U8, name="w_codes", align_bytes=64)
        w_plane = keep.tile([P, E + 1, K], U8, name="w_plane", align_bytes=64)
        ident = keep.tile([P, P], F32, name="ident")

        nc.vector.memset(w_plane[:].bitcast(I32), 0)
        make_identity(nc, ident[:])

        def load_plane(t):
            nc.sync.dma_start(out=planes[t][:], in_=dy_rows[:, t, :])

        def load_gate(lo, hi):
            nc.sync.dma_start(out=gate_sb[:, lo:hi], in_=gate[0:P, lo:hi])

        def load_shared(i):
            nc.sync.dma_start(out=dy_shared[i][:], in_=dy_rows[:, :, i * SHARED_PIECE : (i + 1) * SHARED_PIECE])

        def load_weights():
            nc.sync.dma_start(out=w_codes[:].bitcast(I32), in_=w_words.rearrange("e a p b -> p (e a) b").bitcast(I32))
            scale_rows = w_scales.rearrange("e a f k -> f (e a) k").bitcast(I32)
            for r in range(4):
                nc.sync.dma_start(out=w_plane[r:P:32].bitcast(I32), in_=scale_rows[r:16:4])

        load_plane(0)
        nc.sync.dma_start(offs_sb[:], offs)
        for lo, hi in zip(FIRST_CUTS, FIRST_CUTS[1:]):
            load_gate(lo, hi)
        load_plane(1)
        load_plane(2)
        load_shared(0)
        load_plane(3)
        for i in range(1, 4):
            load_shared(i)
        load_gate(starts[1], starts[2])
        for i in range(4, 6):
            load_shared(i)
        load_weights()
        load_gate(starts[2], S)
        for i in range(6, n_shared):
            load_shared(i)
        nc.sync.dma_start(pos1_sb[:], pos1)
        nc.sync.dma_start(pos2_sb[:], pos2)

        last = (E - 1) * C
        g_f32 = [keep.tile([P, PACK, n], F32, name=f"g_f32_{i}", tag=f"g_f32_{i}" if i < 2 else f"pair{i - 2}", align_bytes=64) for i, n in enumerate(CHUNKS)]
        g_bf_pairs = [keep.tile([P, 2 * C, PACK], BF16, name=f"g_bf_pair{u}", tag=f"pair{u}", align_bytes=64) for u in range(3)]
        g_bf_pairs.append(keep.tile([P, C, PACK], BF16, name="g_bf_6", align_bytes=64))
        g_bf_last = keep.tile([P, C, PACK], BF16, name="g_bf_last", tag="after_last_quantize", align_bytes=64)
        g_codes_main = keep.tile([P, last], U32, name="g_codes_main", align_bytes=64)
        g_codes_last = keep.tile([P, C], U32, name="g_codes_last", tag="after_last_product", align_bytes=64)
        g_plane = keep.tile([P, S], U8, name="g_plane", align_bytes=64)
        dx = keep.tile([P, S], F32, name="dx")

        def g_bf(lo, hi):
            base = lo // (2 * C) * 2 * C
            return g_bf_pairs[lo // (2 * C)][:, lo - base : hi - base, :] if lo < last else g_bf_last[:, lo - last : hi - last, :]

        def g_codes(lo, hi):
            return g_codes_main[:, lo:hi] if lo < last else g_codes_last[:, lo - last : hi - last]

        def gather_g(i, t, lo, hi):
            a, b = starts[i] + lo, starts[i] + hi
            nc.vector.tensor_tensor(
                g_f32[i][:, t, lo:hi], planes[t][:].indirect(offs_sb[:, a // PER_COL : b // PER_COL]), gate_sb[:, a:b], MULT
            )

        def interleave(dst, src):
            nc.scalar.copy(
                out=dst.rearrange("p (c i) t -> p c t i", i=LINE), in_=src.rearrange("p t (c i) -> p c t i", i=LINE)
            )

        def quantize(codes, plane, values):
            nc.vector.quantize_mx(out=codes.bitcast(E5M2), scales=plane, in_=values.rearrange("p c t -> p (c t)"))

        def multiply(e, codes, plane, acc):
            nc.tensor.matmul_mx(
                out=acc[:],
                lhsT=w_codes[:, e, :].bitcast(E2M1),
                lhsT_scale=w_plane[:, e, :],
                rhs=codes.bitcast(E5M2),
                rhs_scale=plane,
                start=True,
                stop=True,
            )

        def multiply_into(e, codes, plane, dst):
            acc = psum.tile([P, C], F32, name="acc", tag="acc", bufs=2)
            multiply(e, codes, plane, acc)
            nc.scalar.copy(out=dst, in_=acc[:])

        def quantize_slots(lo, hi):
            quantize(g_codes(lo, hi), g_plane[:, lo:hi], g_bf(lo, hi))
            for e in range(lo // C, hi // C):
                cols = slice(e * C, (e + 1) * C)
                multiply_into(e, g_codes(cols.start, cols.stop), g_plane[:, cols], dx[:, cols])

        n_groups = T // GROUP
        tail = n_groups - 1
        per_group = GROUP // SHARED_PIECE
        s_bf_early = keep.tile([P, tail * GROUP, PACK], BF16, name="s_bf_early", align_bytes=64)
        for i in range(tail * per_group):
            interleave(s_bf_early[:, i * SHARED_PIECE : (i + 1) * SHARED_PIECE, :], dy_shared[i][:])

        for i, n in enumerate(CHUNKS):
            for t in range(PACK):
                if i == 0 and t == 0:
                    for lo, hi in zip(FIRST_CUTS, FIRST_CUTS[1:]):
                        gather_g(i, t, lo, hi)
                else:
                    gather_g(i, t, 0, n)
                if t == PACK - 1:
                    cuts = sorted({starts[i], starts[i + 1], *range(-(-starts[i] // C) * C, starts[i + 1], C)})
                    for lo, hi in zip(cuts, cuts[1:]):
                        interleave(g_bf(lo, hi), g_f32[i][:, :, lo - starts[i] : hi - starts[i]])
                for lo, hi, chunk, plane in QUANTS:
                    if (chunk, plane) == (i, t):
                        quantize_slots(lo, hi)

        s_plane = keep.tile([P, T], U8, name="s_plane", align_bytes=64)
        s_codes_0 = keep.tile([P, GROUP], U32, name="s_codes_0", tag="plane2", align_bytes=64)
        s_codes_12 = keep.tile([P, 2 * GROUP], U32, name="s_codes_12", tag="after_last_quantize", align_bytes=64)
        s_codes_3 = keep.tile([P, GROUP], U32, name="s_codes_3", tag="plane1", align_bytes=64)
        quantize(s_codes_0[:], s_plane[:, 0:GROUP], s_bf_early[:, 0:GROUP, :])
        quantize(s_codes_12[:], s_plane[:, GROUP : tail * GROUP], s_bf_early[:, GROUP : tail * GROUP, :])
        s_codes = [s_codes_0[:], s_codes_12[:, 0:GROUP], s_codes_12[:, GROUP : 2 * GROUP]]
        ds = [keep.tile([P, GROUP], F32, name=f"ds{q}", tag=f"after_ds{q}")[:] for q in range(tail)]
        for q in range(tail):
            multiply_into(E, s_codes[q], s_plane[:, q * GROUP : (q + 1) * GROUP], ds[q])
        s_bf_tail = keep.tile([P, GROUP, PACK], BF16, name="s_bf_tail", tag="after_last_product", align_bytes=64)
        for h in range(per_group):
            interleave(s_bf_tail[:, h * SHARED_PIECE : (h + 1) * SHARED_PIECE, :], dy_shared[tail * per_group + h][:])

        head = tail * GROUP
        first = keep.tile([P, head], F32, name="first", tag="plane3", align_bytes=64)
        second_0 = keep.tile([P, GROUP], F32, name="second_0", tag="after_ds1")
        second_12 = keep.tile([P, 2, GROUP], F32, name="second_12", tag="after_ds2")
        second = [second_0[:], second_12[:, 0, :], second_12[:, 1, :]]
        tail_pair = keep.tile([P, 2, GROUP], F32, name="tail_pair", tag="after_last_product", align_bytes=64)
        turned = [psum.tile([P, GROUP], F32, name=f"turned{q}") for q in range(tail)]
        blocks = GROUP // P

        def gather_dx(dst, pos_sb, lo, hi):
            nc.vector.tensor_copy(dst, dx[:].indirect(pos_sb[:, lo // PER_COL : hi // PER_COL]))

        def turn(bank, src, start, stop):
            for j in range(blocks):
                nc.tensor.matmul(
                    bank[:, j * P : (j + 1) * P],
                    src[:, j * P : (j + 1) * P],
                    ident[:],
                    start=start and j == 0,
                    stop=stop and j == blocks - 1,
                    is_transpose=True,
                )

        for q in range(tail):
            turn(turned[q], ds[q], True, False)
        for q in range(tail):
            gather_dx(first[:, q * GROUP : (q + 1) * GROUP], pos1_sb, q * GROUP, (q + 1) * GROUP)
            turn(turned[q], first[:, q * GROUP : (q + 1) * GROUP], False, False)
        for q in range(tail):
            gather_dx(second[q], pos2_sb, q * GROUP, (q + 1) * GROUP)
        tail_cols = slice(head, T)
        quantize(s_codes_3[:], s_plane[:, tail_cols], s_bf_tail[:])
        ds_tail = psum.tile([P, GROUP], F32, name="ds_tail")
        multiply(E, s_codes_3[:], s_plane[:, tail_cols], ds_tail)
        gather_dx(tail_pair[:, 0, :], pos1_sb, head, T)
        gather_dx(tail_pair[:, 1, :], pos2_sb, head, T)
        sums = [keep.tile([P, GROUP], F32, name=f"sums{q}", tag=f"stage{q}") for q in range(tail)]
        backs = {}
        for step in range(tail + 1):
            q = step - 1
            if step < tail:
                turn(turned[step], second[step], False, True)
            if q >= 0:
                backs[q] = psum.tile([P, GROUP], F32, name="back", tag="back", bufs=2)
                for j in range(blocks):
                    nc.tensor.transpose(backs[q][:, j * P : (j + 1) * P], sums[q][:, j * P : (j + 1) * P], ident[:])
            if step < tail:
                nc.scalar.copy(out=sums[step][:], in_=turned[step][:])
            if q >= 0:
                result = keep.tile([P, GROUP], F32, name=f"result{q}", tag=f"stage{tail + q}")
                nc.scalar.copy(out=result[:], in_=backs[q][:])
                nc.sync.dma_start(out=out[:, q * GROUP : (q + 1) * GROUP], in_=result[:])
        half = GROUP // 2
        partial = keep.tile([P, GROUP], F32, name="partial", tag="g_f32_0", align_bytes=64)
        result = keep.tile([P, GROUP], F32, name="result_tail", tag="g_f32_1", align_bytes=64)
        for h in range(2):
            cols = slice(h * half, (h + 1) * half)
            nc.vector.tensor_tensor(partial[:, cols], ds_tail[:, cols], tail_pair[:, 0, cols], ADD)
        for h in range(2):
            cols = slice(h * half, (h + 1) * half)
            nc.vector.tensor_tensor(result[:, cols], partial[:, cols], tail_pair[:, 1, cols], ADD)
            nc.sync.dma_start(out=out[:, tail_cols][:, cols], in_=result[:, cols])
